import numpy as np
import ml_dtypes


def mxq(x, axis, fmt="e4m3"):
    dtype, down = {"e4m3": (ml_dtypes.float8_e4m3fn, 7), "e5m2": (ml_dtypes.float8_e5m2, 14)}[fmt]
    v = np.moveaxis(np.asarray(x, np.float32).astype(ml_dtypes.bfloat16).astype(np.float64), axis, -1)
    blocks = v.reshape(v.shape[:-1] + (-1, 32))
    amax = np.abs(blocks).max(-1, keepdims=True)
    byte = np.maximum(np.where(amax > 0, np.frexp(amax)[1] - 1 + 127, 0) - down, 1)
    scale = np.exp2(byte - 127.0)
    codes = (blocks / scale).astype(np.float32).astype(dtype).astype(np.float64)
    return np.moveaxis((codes * scale).reshape(v.shape), -1, axis)


WIDE = False


def mx_kscale(k):
    if not WIDE:
        return np.ones(k)
    levels = np.array([10, -10, 5, -5, 0])
    if k % 512:
        return np.exp2(np.random.permutation(np.resize(levels, k // 32))).repeat(32)
    a = np.empty((k // 512, 16))
    for p in range(k // 512):
        a[p, :8] = np.random.permutation(np.resize(levels, 8))
        for g in range(8):
            far = levels[np.abs(levels - a[p, g]) >= 10]
            a[p, g + 8] = far[np.random.randint(len(far))]
    return np.exp2(a.ravel()).repeat(32)


def f64(x):
    return np.asarray(x).astype(np.float64)


def striped(idx):
    return np.tile(idx.reshape(-1, 16).T, (8, 1)).astype(np.uint16)


def unstriped(offs):
    return offs[:16].T.reshape(-1).astype(np.int64)


def pack_weight(w):
    k, n = w.shape
    w = f64(np.asarray(w, np.float32).astype(ml_dtypes.bfloat16)).reshape(k // 32, 32, n)
    amax = np.abs(w).max(1)
    byte = np.clip(np.where(amax > 0, np.frexp(amax)[1] - 1 + 127 - 7, 1), 1, 254)
    scaled = (w * np.exp2(127.0 - byte)[:, None, :]).reshape(k, n).astype(np.float32)
    words = np.ascontiguousarray(scaled.reshape(k // 512, 128, 4, n).transpose(0, 1, 3, 2)).astype(ml_dtypes.float8_e4m3fn).view(np.uint8)
    return words, np.ascontiguousarray(byte.astype(np.uint8).reshape(k // 512, 16, n))


def unpack_weight(words, scales):
    g, p, n, _ = words.shape
    vals = np.ascontiguousarray(words).view(ml_dtypes.float8_e4m3fn).astype(np.float64) * np.repeat(np.exp2(scales.astype(np.float64) - 127.0), 8, axis=1)[..., None]
    return vals.transpose(0, 1, 3, 2).reshape(g * 512, n)


def planes(y):
    n, m = y.shape
    v = y.astype(np.float32).astype(ml_dtypes.bfloat16).astype(np.float64).reshape(n // 32, 32, m)
    top = np.abs(v).max(1)
    byte = np.clip(np.where(top > 0, np.frexp(top)[1] - 1 + 127 - 7, 1), 1, 254)
    codes = (v * np.exp2(127.0 - byte)[:, None, :]).reshape(n, m).astype(np.float32).astype(ml_dtypes.float8_e4m3fn).view(np.uint8)
    words = codes.reshape(n // 512, 128, 4, m).transpose(0, 1, 3, 2)
    return np.ascontiguousarray(words), np.ascontiguousarray(byte.astype(np.uint8).reshape(n // 512, 16, m))


def gelu(v):
    return 0.5 * v * (1.0 + np.tanh(np.sqrt(2.0 / np.pi) * (v + 0.044715 * v**3)))


K, T, S, H, N = 512, 1024, 512, 512, 512


def setup_inputs():
    n = np.random.standard_normal
    s = mx_kscale(K)[:, None]
    u = mx_kscale(H)
    packed_xT = pack_weight(n((K, T)) * s)
    packed_w4 = pack_weight(n((H, N)) / np.sqrt(H) / u[:, None])
    return {
        "x_words": packed_xT[0],
        "x_scales": packed_xT[1],
        "eT": (n((K, S)) * s).astype(np.float32),
        "w1": (n((K, H)) / np.sqrt(3 * K) / s * u).astype(np.float32),
        "w2": (n((K, H)) / np.sqrt(3 * K) / s * u).astype(np.float32),
        "w3": (n((K, H)) / np.sqrt(3 * K) / s * u).astype(np.float32),
        "w4_words": packed_w4[0],
        "w4_scales": packed_w4[1],
        "offs": striped(np.random.permutation(T)[:S]),
        "dst": striped(np.random.permutation(T)[:S]),
    }


def reference(x_words, x_scales, eT, w1, w2, w3, w4_words, w4_scales, offs, dst):
    xq = unpack_weight(x_words, x_scales)[:, unstriped(offs)]
    x_dst = unpack_weight(x_words, x_scales)[:, unstriped(dst)]
    eTq = mxq(f64(eT), 0, "e4m3")
    h = gelu(mxq(f64(w1), 0, "e4m3").T @ xq + mxq(f64(w2), 0, "e4m3").T @ x_dst + mxq(f64(w3), 0, "e4m3").T @ eTq)
    out_0 = unpack_weight(w4_words, w4_scales).T @ mxq(h, 0, "e4m3")
    return (out_0,) + planes(out_0)

@@ -1,0 +1,201 @@
+from contextlib import ExitStack
+
+import concourse.mybir as mybir
+
+K, T, S, H, N = 512, 1024, 512, 512, 512
+FLOPS = 2 * S * (3 * K * H + H * N)
+
+F32 = mybir.dt.float32
+BF16 = mybir.dt.bfloat16
+I32 = mybir.dt.int32
+U32 = mybir.dt.uint32
+U16 = mybir.dt.uint16
+U8 = mybir.dt.uint8
+FP8X4 = mybir.dt.float8_e4m3fn_x4
+GELU = mybir.ActivationFunctionType.Gelu_apprx_tanh
+
+P = 128
+PACK = 4
+CHUNK = 128
+CHUNKS = S // CHUNK
+QUADS = 4
+LAG = 4
+HALF = H // 2
+OUT_ON_VECTOR = (0,)
+
+
+def tile_picked_zedge_gelu_po_kernel(
+    tc, x_words, x_scales, eT, w1, w2, w3, w4_words, w4_scales, offs, dst, out_0, out_1, out_2
+):
+    nc = tc.nc
+    with ExitStack() as ctx:
+        lists = ctx.enter_context(tc.tile_pool(name="lists", bufs=1))
+        sb = ctx.enter_context(tc.tile_pool(name="sb", bufs=1))
+        psum = ctx.enter_context(tc.psum_pool(name="psum", bufs=1))
+
+        def tile(shape, dtype, name, tag=None):
+            return sb.tile(shape, dtype, name=name, tag=tag or name, align_bytes=64)
+
+        x_w = tile([P, T], I32, "x_w")
+        x_s = tile([P, T], U8, "x_s")
+        w4_w = tile([P, N], I32, "w4_w")
+        w4_s = tile([P, N], U8, "w4_s")
+        offs_t = lists.tile([P, S // 16], U16, name="offs_t")
+        dst_t = lists.tile([P, S // 16], U16, name="dst_t")
+
+        nc.gpsimd.memset(x_s[:].bitcast(I32), 0)
+        nc.gpsimd.memset(w4_s[:].bitcast(I32), 0)
+
+        nc.sync.dma_start(out=x_w[:], in_=x_words[0].rearrange("p c r -> p (c r)").bitcast(I32))
+        nc.sync.dma_start(offs_t[:], offs)
+        nc.sync.dma_start(dst_t[:], dst)
+        for q in range(QUADS):
+            nc.scalar.dma_start(
+                out=x_s[32 * q : 32 * q + 4, :].bitcast(I32), in_=x_scales[0, 4 * q : 4 * q + 4, :].bitcast(I32)
+            )
+        warm_in = tile([P, 8], F32, "warm_in")
+        warm_out = tile([P, 8], F32, "warm_out")
+        nc.gpsimd.memset(warm_in[:], 0.0)
+        nc.scalar.activation(out=warm_out[:, 0:1], in_=warm_in[:, 0:1], func=GELU)
+        for q in range(QUADS):
+            nc.gpsimd.dma_start(
+                out=w4_s[32 * q : 32 * q + 4, :].bitcast(I32), in_=w4_scales[0, 4 * q : 4 * q + 4, :].bitcast(I32)
+            )
+        w_raw = []
+        for i, w in enumerate((w1, w2, w3)):
+            raw = tile([P, PACK, H], F32, "w_raw%d" % i)
+            nc.sync.dma_start(out=raw[:], in_=w.rearrange("(p j) c -> p j c", j=PACK))
+            w_raw.append(raw)
+        e_raw = []
+        e_rows = eT.rearrange("(p j) c -> p j c", j=PACK)
+        for half in range(2):
+            raw = tile([P, PACK, 2 * CHUNK], F32, "e_raw%d" % half)
+            nc.sync.dma_start(out=raw[:], in_=e_rows[:, :, 2 * CHUNK * half : 2 * CHUNK * (half + 1)])
+            e_raw.append(raw)
+        nc.sync.dma_start(out=w4_w[:], in_=w4_words[0].rearrange("p c r -> p (c r)").bitcast(I32))
+
+        acc = [psum.tile([P, PACK, CHUNK], F32, name="acc%d" % c) for c in range(CHUNKS)]
+        res = [psum.tile([P, PACK, CHUNK], F32, name="res%d" % c) for c in range(CHUNKS)]
+
+        def mm(out, lhs, t, rhs, cols, start, stop):
+            lw, ls = lhs
+            rw, rs = rhs
+            tcols = slice(P * t, P * (t + 1))
+            nc.tensor.matmul_mx(
+                out=out,
+                lhsT=lw[:, tcols].bitcast(FP8X4),
+                lhsT_scale=ls[:, tcols],
+                rhs=rw[:, cols].bitcast(FP8X4),
+                rhs_scale=rs[:, cols],
+                start=start,
+                stop=stop,
+            )
+
+        def quantise(rounded, name):
+            width = rounded.shape[1] // PACK
+            words = tile([P, width], U32, name + "_w")
+            scales = tile([P, width], U8, name + "_s")
+            nc.vector.quantize_mx(out=words[:].bitcast(FP8X4), scales=scales[:], in_=rounded[:])
+            return words, scales
+
+        def gather(window, dtype, lst, name, tag=None):
+            picked = tile([P, S], dtype, name, tag)
+            nc.vector.tensor_copy(picked[:], window.indirect(lst[:]))
+            return picked
+
+        def weight_half(copy, i, half, tag=None):
+            name = "w%d_%d" % (i, half)
+            rounded = tile([P, PACK * HALF], BF16, name + "_bf", tag)
+            copy(
+                out=rounded[:].rearrange("p (t m j) -> p m j t", t=2, j=PACK),
+                in_=w_raw[i][:].rearrange("p j (m t) -> p m j t", t=PACK)[:, :, :, 2 * half : 2 * half + 2],
+            )
+            return quantise(rounded, name)
+
+        def node_passes(wq_half, half, picked, first):
+            for t in range(2):
+                for c in range(CHUNKS):
+                    cols = slice(CHUNK * c, CHUNK * (c + 1))
+                    mm(acc[c][:, 2 * half + t, :], wq_half, t, picked, cols, first and t == 0, False)
+
+        x_words_window = x_w[:].bitcast(U32)
+        src = (gather(x_words_window, U32, offs_t, "src_w"), gather(x_s[:], U8, offs_t, "src_s"))
+        dst_w = gather(x_words_window, U32, dst_t, "dst_w")
+        node_passes(weight_half(nc.scalar.copy, 0, 0), 0, src, True)
+        rcv = (dst_w, gather(x_s[:], U8, dst_t, "dst_s", "w0_0_bf"))
+        node_passes(weight_half(nc.scalar.copy, 0, 1), 1, src, False)
+        node_passes(weight_half(nc.scalar.copy, 1, 0), 0, rcv, False)
+        node_passes(weight_half(nc.vector.tensor_copy, 1, 1, "w0_1_bf"), 1, rcv, False)
+        w3q = [weight_half(nc.scalar.copy, 2, 0), weight_half(nc.vector.tensor_copy, 2, 1, "w1_0_bf")]
+
+        whole = slice(0, CHUNK)
+
+        def edge_features(copy, raw, first, count, tag):
+            rounded = tile([P, PACK * CHUNK * count], BF16, "e_bf%d" % first, tag)
+            copy(
+                out=rounded[:].rearrange("p (g i j) -> p g j i", i=4, j=PACK),
+                in_=raw.rearrange("p j (g i) -> p g j i", i=4),
+            )
+            eq = quantise(rounded, "eq%d" % first)
+            for n in range(count):
+                for t in range(PACK):
+                    cols = slice(CHUNK * n, CHUNK * (n + 1))
+                    mm(acc[first + n][:, t, :], w3q[t // 2], t % 2, eq, cols, False, t == PACK - 1)
+
+        edge_features(nc.scalar.copy, e_raw[0][:, :, 0:CHUNK], 0, 1, "w_raw2")
+        edge_features(nc.vector.tensor_copy, e_raw[0][:, :, CHUNK : 2 * CHUNK], 1, 1, "w2_0_bf")
+
+        edge_features(nc.vector.tensor_copy, e_raw[1][:], 2, 2, "w_raw2")
+        w4d_s = tile([P, N], U8, "w4d_s", "e_raw1")
+        nc.vector.tensor_copy(
+            out=w4d_s[:].rearrange("p (t m) -> p t m", t=PACK), in_=w4_s[:].rearrange("p (m t) -> p t m", t=PACK)
+        )
+        w4d_w = tile([P, N], I32, "w4d_w", "w_raw2")
+        nc.vector.tensor_copy(
+            out=w4d_w[:].rearrange("p (t m) -> p m t", t=PACK), in_=w4_w[:].rearrange("p (m t) -> p m t", t=PACK)
+        )
+
+        out_rows = out_0.rearrange("(p t) n -> p t n", t=PACK)
+        out_words = out_1[0].rearrange("p c r -> p (c r)").bitcast(I32)
+        y_w = tile([P, S], I32, "y_w")
+        y_s = tile([P, S], U8, "y_s")
+
+        def hidden(c):
+            h_bf = tile([P, PACK * CHUNK], BF16, "h_bf%d" % c)
+            nc.scalar.activation(
+                out=h_bf[:].rearrange("p (n t) -> p n t", t=PACK),
+                in_=acc[c][:].rearrange("p t n -> p n t"),
+                func=GELU,
+            )
+            hq = quantise(h_bf, "hq%d" % c)
+            for t in range(PACK):
+                mm(res[c][:, t, :], (w4d_w, w4d_s), t, hq, whole, True, True)
+
+        def result(c):
+            cols = slice(CHUNK * c, CHUNK * (c + 1))
+            y = tile([P, PACK, CHUNK], F32, "y%d" % c)
+            if c in OUT_ON_VECTOR:
+                nc.vector.tensor_copy(out=y[:], in_=res[c][:])
+            else:
+                nc.scalar.copy(out=y[:], in_=res[c][:])
+            nc.sync.dma_start(out=out_rows[:, :, cols], in_=y[:])
+            y_bf = tile([P, PACK * CHUNK], BF16, "y_bf%d" % c)
+            nc.vector.tensor_copy(
+                out=y_bf[:].rearrange("p (g i t) -> p g t i", i=4, t=PACK),
+                in_=y[:].rearrange("p t (g i) -> p g t i", i=4),
+            )
+            nc.vector.quantize_mx(out=y_w[:, cols].bitcast(FP8X4), scales=y_s[:, cols], in_=y_bf[:])
+            if c % 2 == 1:
+                pair = slice(CHUNK * (c - 1), CHUNK * (c + 1))
+                nc.sync.dma_start(out=out_words[:, pair], in_=y_w[:, pair])
+
+        for step in range(CHUNKS + LAG):
+            if step < CHUNKS:
+                hidden(step)
+            if step >= LAG:
+                result(step - LAG)
+        for q in range(QUADS):
+            queue = nc.scalar if q % 2 else nc.sync
+            queue.dma_start(
+                out=out_2[0, 4 * q : 4 * q + 4, :].bitcast(I32), in_=y_s[32 * q : 32 * q + 4, :].bitcast(I32)
+            )

@@ -53,10 +53,6 @@ def tile_picked_zedge_gelu_po_kernel(
             nc.scalar.dma_start(
                 out=x_s[32 * q : 32 * q + 4, :].bitcast(I32), in_=x_scales[0, 4 * q : 4 * q + 4, :].bitcast(I32)
             )
-        warm_in = tile([P, 8], F32, "warm_in")
-        warm_out = tile([P, 8], F32, "warm_out")
-        nc.gpsimd.memset(warm_in[:], 0.0)
-        nc.scalar.activation(out=warm_out[:, 0:1], in_=warm_in[:, 0:1], func=GELU)
         for q in range(QUADS):
             nc.gpsimd.dma_start(
                 out=w4_s[32 * q : 32 * q + 4, :].bitcast(I32), in_=w4_scales[0, 4 * q : 4 * q + 4, :].bitcast(I32)

from contextlib import ExitStack

import concourse.mybir as mybir

K, T, S, H, N = 512, 1024, 512, 512, 512
FLOPS = 2 * S * (3 * K * H + H * N)

F32 = mybir.dt.float32
BF16 = mybir.dt.bfloat16
I32 = mybir.dt.int32
U32 = mybir.dt.uint32
U16 = mybir.dt.uint16
U8 = mybir.dt.uint8
FP8X4 = mybir.dt.float8_e4m3fn_x4
GELU = mybir.ActivationFunctionType.Gelu_apprx_tanh

P = 128
PACK = 4
CHUNK = 128
CHUNKS = S // CHUNK
QUADS = 4
LAG = 4
HALF = H // 2
OUT_ON_VECTOR = (0,)


def tile_picked_zedge_gelu_po_kernel(
    tc, x_words, x_scales, eT, w1, w2, w3, w4_words, w4_scales, offs, dst, out_0, out_1, out_2
):
    nc = tc.nc
    with ExitStack() as ctx:
        lists = ctx.enter_context(tc.tile_pool(name="lists", bufs=1))
        sb = ctx.enter_context(tc.tile_pool(name="sb", bufs=1))
        psum = ctx.enter_context(tc.psum_pool(name="psum", bufs=1))

        def tile(shape, dtype, name, tag=None):
            return sb.tile(shape, dtype, name=name, tag=tag or name, align_bytes=64)

        x_w = tile([P, T], I32, "x_w")
        x_s = tile([P, T], U8, "x_s")
        w4_w = tile([P, N], I32, "w4_w")
        w4_s = tile([P, N], U8, "w4_s")
        offs_t = lists.tile([P, S // 16], U16, name="offs_t")
        dst_t = lists.tile([P, S // 16], U16, name="dst_t")

        nc.gpsimd.memset(x_s[:].bitcast(I32), 0)
        nc.gpsimd.memset(w4_s[:].bitcast(I32), 0)

        nc.sync.dma_start(out=x_w[:], in_=x_words[0].rearrange("p c r -> p (c r)").bitcast(I32))
        nc.sync.dma_start(offs_t[:], offs)
        nc.sync.dma_start(dst_t[:], dst)
        for q in range(QUADS):
            nc.scalar.dma_start(
                out=x_s[32 * q : 32 * q + 4, :].bitcast(I32), in_=x_scales[0, 4 * q : 4 * q + 4, :].bitcast(I32)
            )
        for q in range(QUADS):
            nc.gpsimd.dma_start(
                out=w4_s[32 * q : 32 * q + 4, :].bitcast(I32), in_=w4_scales[0, 4 * q : 4 * q + 4, :].bitcast(I32)
            )
        w_raw = []
        for i, w in enumerate((w1, w2, w3)):
            raw = tile([P, PACK, H], F32, "w_raw%d" % i)
            nc.sync.dma_start(out=raw[:], in_=w.rearrange("(p j) c -> p j c", j=PACK))
            w_raw.append(raw)
        e_raw = []
        e_rows = eT.rearrange("(p j) c -> p j c", j=PACK)
        for half in range(2):
            raw = tile([P, PACK, 2 * CHUNK], F32, "e_raw%d" % half)
            nc.sync.dma_start(out=raw[:], in_=e_rows[:, :, 2 * CHUNK * half : 2 * CHUNK * (half + 1)])
            e_raw.append(raw)
        nc.sync.dma_start(out=w4_w[:], in_=w4_words[0].rearrange("p c r -> p (c r)").bitcast(I32))

        acc = [psum.tile([P, PACK, CHUNK], F32, name="acc%d" % c) for c in range(CHUNKS)]
        res = [psum.tile([P, PACK, CHUNK], F32, name="res%d" % c) for c in range(CHUNKS)]

        def mm(out, lhs, t, rhs, cols, start, stop):
            lw, ls = lhs
            rw, rs = rhs
            tcols = slice(P * t, P * (t + 1))
            nc.tensor.matmul_mx(
                out=out,
                lhsT=lw[:, tcols].bitcast(FP8X4),
                lhsT_scale=ls[:, tcols],
                rhs=rw[:, cols].bitcast(FP8X4),
                rhs_scale=rs[:, cols],
                start=start,
                stop=stop,
            )

        def quantise(rounded, name):
            width = rounded.shape[1] // PACK
            words = tile([P, width], U32, name + "_w")
            scales = tile([P, width], U8, name + "_s")
            nc.vector.quantize_mx(out=words[:].bitcast(FP8X4), scales=scales[:], in_=rounded[:])
            return words, scales

        def gather(window, dtype, lst, name, tag=None):
            picked = tile([P, S], dtype, name, tag)
            nc.vector.tensor_copy(picked[:], window.indirect(lst[:]))
            return picked

        def weight_half(copy, i, half, tag=None):
            name = "w%d_%d" % (i, half)
            rounded = tile([P, PACK * HALF], BF16, name + "_bf", tag)
            copy(
                out=rounded[:].rearrange("p (t m j) -> p m j t", t=2, j=PACK),
                in_=w_raw[i][:].rearrange("p j (m t) -> p m j t", t=PACK)[:, :, :, 2 * half : 2 * half + 2],
            )
            return quantise(rounded, name)

        def node_passes(wq_half, half, picked, first):
            for t in range(2):
                for c in range(CHUNKS):
                    cols = slice(CHUNK * c, CHUNK * (c + 1))
                    mm(acc[c][:, 2 * half + t, :], wq_half, t, picked, cols, first and t == 0, False)

        x_words_window = x_w[:].bitcast(U32)
        src = (gather(x_words_window, U32, offs_t, "src_w"), gather(x_s[:], U8, offs_t, "src_s"))
        dst_w = gather(x_words_window, U32, dst_t, "dst_w")
        node_passes(weight_half(nc.scalar.copy, 0, 0), 0, src, True)
        rcv = (dst_w, gather(x_s[:], U8, dst_t, "dst_s", "w0_0_bf"))
        node_passes(weight_half(nc.scalar.copy, 0, 1), 1, src, False)
        node_passes(weight_half(nc.scalar.copy, 1, 0), 0, rcv, False)
        node_passes(weight_half(nc.vector.tensor_copy, 1, 1, "w0_1_bf"), 1, rcv, False)
        w3q = [weight_half(nc.scalar.copy, 2, 0), weight_half(nc.vector.tensor_copy, 2, 1, "w1_0_bf")]

        whole = slice(0, CHUNK)

        def edge_features(copy, raw, first, count, tag):
            rounded = tile([P, PACK * CHUNK * count], BF16, "e_bf%d" % first, tag)
            copy(
                out=rounded[:].rearrange("p (g i j) -> p g j i", i=4, j=PACK),
                in_=raw.rearrange("p j (g i) -> p g j i", i=4),
            )
            eq = quantise(rounded, "eq%d" % first)
            for n in range(count):
                for t in range(PACK):
                    cols = slice(CHUNK * n, CHUNK * (n + 1))
                    mm(acc[first + n][:, t, :], w3q[t // 2], t % 2, eq, cols, False, t == PACK - 1)

        edge_features(nc.scalar.copy, e_raw[0][:, :, 0:CHUNK], 0, 1, "w_raw2")
        edge_features(nc.vector.tensor_copy, e_raw[0][:, :, CHUNK : 2 * CHUNK], 1, 1, "w2_0_bf")

        edge_features(nc.vector.tensor_copy, e_raw[1][:], 2, 2, "w_raw2")
        w4d_s = tile([P, N], U8, "w4d_s", "e_raw1")
        nc.vector.tensor_copy(
            out=w4d_s[:].rearrange("p (t m) -> p t m", t=PACK), in_=w4_s[:].rearrange("p (m t) -> p t m", t=PACK)
        )
        w4d_w = tile([P, N], I32, "w4d_w", "w_raw2")
        nc.vector.tensor_copy(
            out=w4d_w[:].rearrange("p (t m) -> p m t", t=PACK), in_=w4_w[:].rearrange("p (m t) -> p m t", t=PACK)
        )

        out_rows = out_0.rearrange("(p t) n -> p t n", t=PACK)
        out_words = out_1[0].rearrange("p c r -> p (c r)").bitcast(I32)
        y_w = tile([P, S], I32, "y_w")
        y_s = tile([P, S], U8, "y_s")

        def hidden(c):
            h_bf = tile([P, PACK * CHUNK], BF16, "h_bf%d" % c)
            nc.scalar.activation(
                out=h_bf[:].rearrange("p (n t) -> p n t", t=PACK),
                in_=acc[c][:].rearrange("p t n -> p n t"),
                func=GELU,
            )
            hq = quantise(h_bf, "hq%d" % c)
            for t in range(PACK):
                mm(res[c][:, t, :], (w4d_w, w4d_s), t, hq, whole, True, True)

        def result(c):
            cols = slice(CHUNK * c, CHUNK * (c + 1))
            y = tile([P, PACK, CHUNK], F32, "y%d" % c)
            if c in OUT_ON_VECTOR:
                nc.vector.tensor_copy(out=y[:], in_=res[c][:])
            else:
                nc.scalar.copy(out=y[:], in_=res[c][:])
            nc.sync.dma_start(out=out_rows[:, :, cols], in_=y[:])
            y_bf = tile([P, PACK * CHUNK], BF16, "y_bf%d" % c)
            nc.vector.tensor_copy(
                out=y_bf[:].rearrange("p (g i t) -> p g t i", i=4, t=PACK),
                in_=y[:].rearrange("p t (g i) -> p g t i", i=4),
            )
            nc.vector.quantize_mx(out=y_w[:, cols].bitcast(FP8X4), scales=y_s[:, cols], in_=y_bf[:])
            if c % 2 == 1:
                pair = slice(CHUNK * (c - 1), CHUNK * (c + 1))
                nc.sync.dma_start(out=out_words[:, pair], in_=y_w[:, pair])

        for step in range(CHUNKS + LAG):
            if step < CHUNKS:
                hidden(step)
            if step >= LAG:
                result(step - LAG)
        for q in range(QUADS):
            queue = nc.scalar if q % 2 else nc.sync
            queue.dma_start(
                out=out_2[0, 4 * q : 4 * q + 4, :].bitcast(I32), in_=y_s[32 * q : 32 * q + 4, :].bitcast(I32)
            )
